import numpy as np
import ml_dtypes


def mxq(x, axis, fmt="e4m3"):
    dtype, down = {"e4m3": (ml_dtypes.float8_e4m3fn, 7), "e5m2": (ml_dtypes.float8_e5m2, 14)}[fmt]
    v = np.moveaxis(np.asarray(x, np.float32).astype(ml_dtypes.bfloat16).astype(np.float64), axis, -1)
    blocks = v.reshape(v.shape[:-1] + (-1, 32))
    amax = np.abs(blocks).max(-1, keepdims=True)
    byte = np.maximum(np.where(amax > 0, np.frexp(amax)[1] - 1 + 127, 0) - down, 1)
    scale = np.exp2(byte - 127.0)
    codes = (blocks / scale).astype(np.float32).astype(dtype).astype(np.float64)
    return np.moveaxis((codes * scale).reshape(v.shape), -1, axis)


WIDE = False


def mx_kscale(k):
    if not WIDE:
        return np.ones(k)
    levels = np.array([10, -10, 5, -5, 0])
    if k % 512:
        return np.exp2(np.random.permutation(np.resize(levels, k // 32))).repeat(32)
    a = np.empty((k // 512, 16))
    for p in range(k // 512):
        a[p, :8] = np.random.permutation(np.resize(levels, 8))
        for g in range(8):
            far = levels[np.abs(levels - a[p, g]) >= 10]
            a[p, g + 8] = far[np.random.randint(len(far))]
    return np.exp2(a.ravel()).repeat(32)


BF16 = ml_dtypes.bfloat16


def bf(x):
    return np.asarray(x, np.float32).astype(BF16)


def f64(x):
    return np.asarray(x).astype(np.float64)


E2M1 = np.array([0.0, 0.5, 1.0, 1.5, 2.0, 3.0, 4.0, 6.0, -0.0, -0.5, -1.0, -1.5, -2.0, -3.0, -4.0, -6.0])


def pack_weight(w, fmt):
    k, n = w.shape
    w = f64(bf(w)).reshape(k // 32, 32, n)
    amax = np.abs(w).max(1)
    if fmt == "e4m3":
        byte = np.frexp(amax)[1] - 1 + 127 - 7
    else:
        mant, ex = np.frexp(amax / 6.0)
        byte = np.where(mant > 0.5, ex, ex - 1) + 127
    byte = np.clip(np.where(amax > 0, byte, 1), 1, 254)
    scaled = (w * np.exp2(127.0 - byte)[:, None, :]).reshape(k, n).astype(np.float32)
    by_word = np.ascontiguousarray(scaled.reshape(k // 512, 128, 4, n).transpose(0, 1, 3, 2))
    if fmt == "e4m3":
        words = by_word.astype(ml_dtypes.float8_e4m3fn).view(np.uint8)
    else:
        c = by_word.astype(ml_dtypes.float4_e2m1fn).view(np.uint8) & 0xF
        words = c[..., 0::2] | (c[..., 1::2] << 4)
    return np.ascontiguousarray(words), np.ascontiguousarray(byte.astype(np.uint8).reshape(k // 512, 16, n))


def unpack_weight(words, scales, fmt):
    g, p, n, _ = words.shape
    if fmt == "e4m3":
        vals = np.ascontiguousarray(words).view(ml_dtypes.float8_e4m3fn).astype(np.float64)
    else:
        nib = np.empty((g, p, n, 4), np.uint8)
        nib[..., 0::2] = words & 0xF
        nib[..., 1::2] = words >> 4
        vals = E2M1[nib]
    vals = vals * np.repeat(np.exp2(scales.astype(np.float64) - 127.0), 8, axis=1)[..., None]
    return vals.transpose(0, 1, 3, 2).reshape(g * 512, n)
def pack4(w):
    words, scales = pack_weight(w, "e2m1")
    return words.reshape(words.shape[0], 128, -1), scales


def unpack4(words, scales):
    return unpack_weight(words.reshape(words.shape[0], 128, -1, 2), scales, "e2m1")


M, D, F, C, R = 2048, 1024, 1024, 1024, 8


def setup_inputs():
    s, t = mx_kscale(D), mx_kscale(F)
    x = np.random.standard_normal((M, D)) * s
    w = np.random.standard_normal((D, F)) / np.sqrt(D) / s[:, None] * t
    l = np.random.standard_normal((F, R)) / np.sqrt(F)
    sigma = np.sum(l[:, None, :] * l[None, :, :], axis=2) + np.eye(F) / F
    sigma = sigma / t[:, None] / t
    x_words, x_scales = pack4(x.T)
    w_words, w_scales = pack4(w)
    sigma_words, sigma_scales = pack_weight(sigma, "e4m3")
    return {"x_words": x_words, "x_scales": x_scales,
            "w_words": w_words, "w_scales": w_scales,
            "sigma_words": sigma_words, "sigma_scales": sigma_scales,
            "logits": bf(3.0 * np.random.standard_normal((M, C)))}


def reference(x_words, x_scales, w_words, w_scales, sigma_words, sigma_scales, logits):
    xt = unpack4(x_words, x_scales)
    w = unpack4(w_words, w_scales)
    sigma = unpack_weight(sigma_words, sigma_scales, "e4m3")
    phi = np.maximum(xt.T @ w, 0.0)
    v = mxq(phi, 1, "e4m3") @ sigma
    a = np.sum(v * phi, axis=1, keepdims=True)
    out = f64(logits) / np.sqrt(1.0 + a)
    return out, a

from contextlib import ExitStack

import concourse.mybir as mybir
from concourse.masks import make_identity

SAMPLES, D, F, CLASSES = 2048, 1024, 1024, 1024
FLOPS = 2 * SAMPLES * F * D + 2 * SAMPLES * F * F

F32 = mybir.dt.float32
BF16 = mybir.dt.bfloat16
I32 = mybir.dt.int32
U32 = mybir.dt.uint32
U8 = mybir.dt.uint8
FP8X4 = mybir.dt.float8_e4m3fn_x4
FP4X4 = mybir.dt.float4_e2m1fn_x4
ACT = mybir.ActivationFunctionType
ALU = mybir.AluOpType
AX = mybir.AxisListType

P = 128
KG = 2
TILES = 8
BANK = 512
GROUPS = (256,) * 8
KEEP = (5, 5, 5, 5, 5, 5, 5, 8)
V_CASTS = (3,) * 8
LAG2 = (5, 5, 4, 4, 4, 4, 4, 4)
DC = 0
DQ = 2
DF = 2
DT = 4
DV = 5
DE = 6
DL = 0
LASTV = (2, 2, 3)
X_LOADS = ((0, 1), (1, 4), (4, 8))


def tile_laplace_probit_logits_s4_kernel(
    tc, x_words, x_scales, w_words, w_scales, sigma_words, sigma_scales, logits, out_0, out_1
):
    nc = tc.nc
    with ExitStack() as ctx:
        keep = ctx.enter_context(tc.tile_pool(name="keep", bufs=1))
        work = ctx.enter_context(tc.tile_pool(name="work", bufs=2))
        outs = ctx.enter_context(tc.tile_pool(name="outs", bufs=4))
        ps1 = ctx.enter_context(tc.psum_pool(name="ps1", bufs=3))
        ps2 = ctx.enter_context(tc.psum_pool(name="ps2", bufs=3))
        ps3 = ctx.enter_context(tc.psum_pool(name="ps3", bufs=2))
        ctx.enter_context(tc.manual_schedule())

        starts = [sum(GROUPS[:s]) for s in range(len(GROUPS))]

        w_raw = [keep.tile([P, KG, 1024], U8, align_bytes=64, name="w_raw%d" % g) for g in range(2)]
        w_q = [keep.tile([P, KG, 4, 256], U8, align_bytes=64, name="w_q%d" % g) for g in range(2)]
        ws_raw = keep.tile([P, KG, F], U8, align_bytes=64, name="ws_raw")
        ws_q = [keep.tile([P, KG, 4, P], U8, align_bytes=64, name="ws_q%d" % g) for g in range(2)]
        s_raw = [keep.tile([P, F], I32, align_bytes=64, name="s_raw%d" % g) for g in range(KG)]
        s_q = [keep.tile([P, TILES, P], I32, align_bytes=64, name="s_q%d" % g) for g in range(KG)]
        ss_raw = keep.tile([P, KG, F], U8, align_bytes=64, name="ss_raw")
        ss_q = [keep.tile([P, TILES, P], U8, align_bytes=64, name="ss_q%d" % g) for g in range(KG)]
        x_q = [keep.tile([P, KG, 512 * (b - a)], U8, align_bytes=64, name="x_q%d" % a) for a, b in X_LOADS]
        xs = keep.tile([P, KG, SAMPLES], U8, align_bytes=64, name="xs")
        lg = [keep.tile([P, 2, CLASSES], BF16, name="lg%d" % i) for i in range(SAMPLES // P // 2)]
        ident = keep.tile([P, P], F32, name="ident")
        a_cols = keep.tile([P, P], F32, name="a_cols")
        r_cols = keep.tile([P, SAMPLES // P], F32, name="r_cols")
        dummy = keep.tile([P, 1], F32, name="dummy")

        def fill_scales(eng, plane, rows):
            for q in range(4):
                eng.dma_start(
                    out=plane[32 * q : 32 * q + 4, :, :].bitcast(I32),
                    in_=rows[:, 4 * q : 4 * q + 4, :].rearrange("g q n -> q g n").bitcast(I32),
                )

        def zero(eng, tile3):
            eng.memset(tile3[:].rearrange("p g n -> p (g n)").bitcast(I32), 0)

        def load_w(g):
            nc.sync.dma_start(out=w_raw[g][:], in_=w_words[:, :, 1024 * g : 1024 * (g + 1)].rearrange("g p b -> p g b"))

        def load_x(i):
            a, b = X_LOADS[i]
            nc.sync.dma_start(out=x_q[i][:], in_=x_words[:, :, 512 * a : 512 * b].rearrange("g p b -> p g b"))

        zero(nc.vector, ws_raw)
        zero(nc.vector, xs)
        zero(nc.gpsimd, ss_raw)
        nc.gpsimd.memset(dummy[:], 0.0)
        nc.gpsimd.memset(a_cols[:], 0.0)
        load_w(0)
        load_x(0)
        fill_scales(nc.scalar, ws_raw, w_scales)
        fill_scales(nc.scalar, xs, x_scales)
        nc.scalar.activation(dummy[:], dummy[:], ACT.Abs_reciprocal_sqrt, bias=1.0)
        load_w(1)
        load_x(1)
        fill_scales(nc.sync, ss_raw, sigma_scales)
        for g in range(KG):
            nc.sync.dma_start(out=s_raw[g][:], in_=sigma_words[g].rearrange("p n t -> p (n t)").bitcast(I32))
        load_x(2)
        for i in range(SAMPLES // P // 2):
            nc.sync.dma_start(out=lg[i][:], in_=logits[2 * P * i : 2 * P * (i + 1), :].rearrange("(j p) c -> p j c", p=P))
        make_identity(nc, ident[:])

        def order_ws(g):
            for kg in range(KG):
                nc.vector.tensor_copy(
                    out=ws_q[g][:, kg, :, :],
                    in_=ws_raw[:, kg, 512 * g : 512 * (g + 1)].rearrange("p (m t) -> p t m", t=4),
                )

        def order_w(g):
            for t in range(4):
                nc.vector.tensor_copy(
                    out=w_q[g][:, :, t, :].rearrange("p g (m b) -> p g m b", b=2),
                    in_=w_raw[g][:].rearrange("p g (m t b) -> p g t m b", t=4, b=2)[:, :, t, :, :],
                )

        def order_sigma(kg):
            nc.vector.tensor_copy(
                out=ss_q[kg][:].rearrange("p (g t) m -> p g t m", t=4),
                in_=ss_raw[:, kg, :].rearrange("p (g m t) -> p g t m", t=4, m=P),
            )
            nc.vector.tensor_copy(
                out=s_q[kg][:].rearrange("p (g t) m -> p g t m", t=4),
                in_=s_raw[kg][:].rearrange("p (g m t) -> p g t m", t=4, m=P),
            )

        phi, prod, codes, cscale, xb = {}, {}, {}, {}, {}
        units = []
        for s, n in enumerate(GROUPS):
            for b in range(TILES * n // BANK):
                units.append((s, b))
        agenda = {}

        def at(step, fn, *args):
            agenda.setdefault(step, []).append((fn, args))

        def x_words_of(s, kg):
            for i, (a, b) in enumerate(X_LOADS):
                if a <= s < b:
                    return x_q[i][:, kg, 512 * (s - a) : 512 * (s - a + 1)]

        def x_scale(s, kg):
            return xs[:, kg, starts[s] : starts[s] + GROUPS[s]]

        banks1, banks2, banks3 = {}, {}, {}

        def tiles_of(s, b):
            per = BANK // GROUPS[s]
            return per, range(per * b, per * (b + 1))

        def stage1(s, b):
            n = GROUPS[s]
            per, ts = tiles_of(s, b)
            h = ps1.tile([P, per, n], F32, name="h")
            banks1[s, b] = h
            for i, t in enumerate(ts):
                for kg in range(KG):
                    nc.tensor.matmul_mx(
                        out=h[:, i, :],
                        lhsT=w_q[t // 4][:, kg, t % 4, :].bitcast(FP4X4),
                        lhsT_scale=ws_q[t // 4][:, kg, t % 4, :],
                        rhs=x_words_of(s, kg).bitcast(FP4X4),
                        rhs_scale=x_scale(s, kg),
                        start=(kg == 0),
                        stop=(kg == KG - 1),
                    )

        def leave1(s, b):
            n = GROUPS[s]
            per, ts = tiles_of(s, b)
            if b == 0:
                phi[s] = work.tile([P, TILES, n], F32, name="phi", bufs=3)
            nc.scalar.activation(
                phi[s][:, ts[0] : ts[0] + per, :].rearrange("p t n -> p (t n)"),
                banks1[s, b][:].rearrange("p t n -> p (t n)"),
                ACT.Relu,
            )

        def cast(s, g, c):
            n = GROUPS[s]
            if c == 0:
                xb[s, g] = work.tile([P, n, 4], BF16, align_bytes=64, name="xb", bufs=3)
            cols = slice(n // 2 * c, n // 2 * (c + 1))
            dst = xb[s, g][:, cols, :].rearrange("p (c i) t -> p c t i", i=4)
            srcv = phi[s][:, 4 * g : 4 * g + 4, cols].rearrange("p t (c i) -> p c t i", i=4)
            if 2 * g + c < V_CASTS[s]:
                nc.vector.tensor_copy(out=dst, in_=srcv)
            else:
                nc.scalar.copy(dst, srcv)

        def quant(s, g):
            n = GROUPS[s]
            if g == 0:
                codes[s] = work.tile([P, KG, n], U32, align_bytes=64, name="codes", bufs=2)
                cscale[s] = work.tile([P, KG, n], U8, align_bytes=64, name="cscale", bufs=2)
            nc.vector.quantize_mx(
                out=codes[s][:, g, :].bitcast(FP8X4),
                scales=cscale[s][:, g, :],
                in_=xb[s, g][:].rearrange("p n t -> p (n t)"),
            )

        def stage2(s, b):
            n = GROUPS[s]
            per, ts = tiles_of(s, b)
            v = ps2.tile([P, per, n], F32, name="v")
            banks2[s, b] = v
            for i, t in enumerate(ts):
                for g in range(KG):
                    nc.tensor.matmul_mx(
                        out=v[:, i, :],
                        lhsT=s_q[g][:, t, :].bitcast(FP8X4),
                        lhsT_scale=ss_q[g][:, t, :],
                        rhs=codes[s][:, g, :].bitcast(FP8X4),
                        rhs_scale=cscale[s][:, g, :],
                        start=(g == 0),
                        stop=(g == KG - 1),
                    )

        def leave2(s, b):
            n = GROUPS[s]
            per, ts = tiles_of(s, b)
            if b == 0:
                prod[s] = work.tile([P, TILES, n], F32, name="prod", bufs=2)
            rng = slice(ts[0], ts[0] + per)
            nc.vector.tensor_tensor(
                out=prod[s][:, rng, :].rearrange("p t n -> p (t n)"),
                in0=banks2[s, b][:].rearrange("p t n -> p (t n)"),
                in1=phi[s][:, rng, :].rearrange("p t n -> p (t n)"),
                op=ALU.mult,
            )

        def fold(s, t):
            nc.vector.tensor_tensor(
                out=prod[s][:, t - KEEP[s], :], in0=prod[s][:, t - KEEP[s], :], in1=prod[s][:, t, :], op=ALU.add
            )

        def turn(s):
            j_n = GROUPS[s] // P
            tr = ps3.tile([P, 4, P], F32, name="tr")
            banks3[s] = tr
            for j in range(j_n):
                for t in range(KEEP[s]):
                    nc.tensor.matmul(
                        tr[:, j, :],
                        lhsT=prod[s][:, t, P * j : P * (j + 1)],
                        rhs=ident[:],
                        start=(t == 0),
                        stop=(t == KEEP[s] - 1),
                        is_transpose=True,
                    )

        def variance(s):
            j0, j_n = starts[s] // P, GROUPS[s] // P
            nc.vector.reduce_sum(out=a_cols[:, j0 : j0 + j_n], in_=banks3[s][:, 0:j_n, :], axis=AX.X)
            nc.scalar.activation(
                r_cols[:, j0 : j0 + j_n], a_cols[:, j0 : j0 + j_n], ACT.Abs_reciprocal_sqrt, bias=1.0
            )

        def emit(i):
            o = outs.tile([P, CLASSES], F32, name="o")
            nc.scalar.activation(o[:], lg[i // 2][:, i % 2, :], ACT.Copy, scale=r_cols[:, i : i + 1])
            nc.sync.dma_start(out=out_0[P * i : P * (i + 1), :], in_=o[:])

        def emit_halves(i):
            half = CLASSES // 2
            o_s = outs.tile([P, half], F32, name="o_s", bufs=2)
            nc.scalar.activation(o_s[:], lg[i // 2][:, i % 2, 0:half], ACT.Copy, scale=r_cols[:, i : i + 1])
            o_v = outs.tile([P, half], F32, name="o_v", bufs=2)
            nc.vector.tensor_scalar_mul(o_v[:], lg[i // 2][:, i % 2, half:CLASSES], r_cols[:, i : i + 1])
            nc.sync.dma_start(out=out_0[P * i : P * (i + 1), half:CLASSES], in_=o_v[:])
            nc.sync.dma_start(out=out_0[P * i : P * (i + 1), 0:half], in_=o_s[:])

        def store_a():
            ta = ps3.tile([P, 4, P], F32, name="tr")
            nc.tensor.transpose(ta[:, 0, :], a_cols[:], ident[:])
            rows = keep.tile([SAMPLES // P, P], F32, name="a_rows")
            nc.scalar.copy(rows[:], ta[0 : SAMPLES // P, 0, :])
            nc.sync.dma_start(out=out_1.rearrange("(j p) o -> j (p o)", p=P), in_=rows[:])

        ends = {}
        for k, (s, b) in enumerate(units):
            ends[s] = k
        order_ws(0)
        order_w(0)
        queue2 = list(units)
        k = 0
        while k < len(units) or queue2 or [st for st in agenda if st >= k]:
            if k < len(units):
                s, b = units[k]
                stage1(s, b)
            if queue2 and k >= ends[queue2[0][0]] + LAG2[queue2[0][0]]:
                s2, b2 = queue2.pop(0)
                stage2(s2, b2)
                at(k + DL, leave2, s2, b2)
                per, ts = tiles_of(s2, b2)
                for t in ts:
                    if t >= KEEP[s2]:
                        at(k + DF, fold, s2, t)
                if ts[-1] == TILES - 1:
                    last = not queue2
                    dt, dv, de = LASTV if last else (DT, DV, DE)
                    at(k + dt, turn, s2)
                    at(k + dv, variance, s2)
                    for j in range(GROUPS[s2] // P):
                        i = starts[s2] // P + j
                        if last:
                            at(k + de, emit_halves, i)
                        else:
                            at(k + de + (j if s2 < 6 else 0), emit, i)
                    if last:
                        at(k + de, store_a)
            if k < len(units):
                leave1(s, b)
                per, ts = tiles_of(s, b)
                if (ts[-1] + 1) % 4 == 0:
                    g = ts[-1] // 4
                    at(k + DC, cast, s, g, 0)
                    at(k + DC, cast, s, g, 1)
                    at(k + DQ, quant, s, g)
            for fn, args in agenda.pop(k, []):
                fn(*args)
            if k == 0:
                order_ws(1)
                order_w(1)
            if k in (1, 2):
                order_sigma(k - 1)
            k += 1
